import numpy as np
import ml_dtypes

BF16 = ml_dtypes.bfloat16


def bf(x):
    return np.asarray(x, np.float32).astype(BF16)


def f32(x):
    return np.asarray(x, np.float32)


def f64(x):
    return np.asarray(x).astype(np.float64)


def striped(idx):
    return np.tile(idx.reshape(-1, 16).T, (8, 1))


def rows(idx, k):
    return np.tile(idx, (k, 1))


def look(tab, idx):
    return np.take_along_axis(f64(tab), rows(idx, len(tab)), axis=1)


K, S, V, N, M = 256, 2048, 512, 512, 512


def setup_inputs():
    return {"tab": f32(np.random.standard_normal((2, K, S))), "w": bf(np.random.standard_normal((K, M)) / np.sqrt(K)), "b": f32(0.5 * np.random.standard_normal((M, 1))), "offs": striped(np.random.permutation(S)[:N])}


def reference(tab, w, b, offs):
    idx = offs[:16].T.reshape(-1)
    x = (look(tab[0], idx) >= 0.25) * 0.5 * np.tanh(look(tab[1], idx))
    return np.maximum(f64(w).T @ x + f64(b), 0.0)

@@ -1,0 +1,62 @@
+import concourse.mybir as mybir
+
+BF16, F32, U16 = mybir.dt.bfloat16, mybir.dt.float32, mybir.dt.uint16
+ALU = mybir.AluOpType
+ACT = mybir.ActivationFunctionType
+
+P = 128
+ROWS, PLACES = 256, 2048
+PICKS, OUTS = 512, 512
+THRESHOLD, GAIN = 0.25, 0.5
+FLOPS = 2 * ROWS * OUTS * PICKS
+
+
+def tile_lookup_steptanh_relu_kernel(tc, tab, w, b, offs, out):
+    nc = tc.nc
+    row_blocks = ROWS // P
+    out_blocks = OUTS // P
+    out_by_block = out.rearrange("(p c) j -> c p j", c=out_blocks)
+    with (
+        tc.tile_pool(name="held", bufs=1) as held,
+        tc.psum_pool(name="psum", bufs=1) as psum,
+    ):
+        offsets = held.tile([P, PICKS // 16], U16, name="offsets")
+        nc.sync.dma_start(offsets[:], offs)
+
+        weights = held.tile([P, row_blocks, OUTS], BF16, name="weights")
+        bias = held.tile([P, out_blocks], F32, name="bias")
+        keys, values = [], []
+        for r in range(row_blocks):
+            rows = slice(r * P, (r + 1) * P)
+            key = held.tile([P, PLACES], F32, name=f"key{r}")
+            value = held.tile([P, PLACES], F32, name=f"value{r}")
+            nc.sync.dma_start(key[:], tab[0, rows, :])
+            nc.sync.dma_start(value[:], tab[1, rows, :])
+            if r == 0:
+                nc.sync.dma_start(weights[:], w.rearrange("(r p) m -> p r m", p=P))
+                nc.sync.dma_start(bias[:], b.rearrange("(p c) one -> p (c one)", c=out_blocks))
+            keys.append(key)
+            values.append(value)
+
+        sums = [psum.tile([P, PICKS], F32, name=f"sums{c}") for c in range(out_blocks)]
+        for r in range(row_blocks):
+            gate = held.tile([P, PICKS], F32, name=f"gate{r}")
+            squashed = held.tile([P, PICKS], F32, name=f"squashed{r}")
+            x = held.tile([P, PICKS], BF16, name=f"x{r}")
+            nc.vector.tensor_scalar(gate[:], keys[r][:].indirect(offsets[:]), THRESHOLD, GAIN, ALU.is_ge, ALU.mult)
+            nc.scalar.activation(squashed[:], values[r][:].indirect(offsets[:]), ACT.Tanh)
+            nc.vector.tensor_tensor(x[:], gate[:], squashed[:], ALU.mult)
+            for c in range(out_blocks):
+                nc.tensor.matmul(
+                    sums[c][:], weights[:, r, c::out_blocks], x[:],
+                    start=(r == 0), stop=(r == row_blocks - 1),
+                )
+
+        for c in range(out_blocks):
+            result = held.tile([P, PICKS], F32, name=f"result{c}")
+            bias_c = bias[:, c : c + 1]
+            if c % 2 == 0:
+                nc.scalar.activation(result[:], sums[c][:], ACT.Relu, bias=bias_c)
+            else:
+                nc.vector.tensor_scalar(result[:], sums[c][:], bias_c, 0.0, ALU.add, ALU.max)
+            nc.sync.dma_start(out_by_block[c], result[:])

@@ -7,6 +7,8 @@ ACT = mybir.ActivationFunctionType
 P = 128
 ROWS, PLACES = 256, 2048
 PICKS, OUTS = 512, 512
+PARTS = 2
+PART = PICKS // PARTS
 THRESHOLD, GAIN = 0.25, 0.5
 FLOPS = 2 * ROWS * OUTS * PICKS
 
@@ -15,7 +17,7 @@ def tile_lookup_steptanh_relu_kernel(tc, tab, w, b, offs, out):
     nc = tc.nc
     row_blocks = ROWS // P
     out_blocks = OUTS // P
-    out_by_block = out.rearrange("(p c) j -> c p j", c=out_blocks)
+    out_by_part = out.rearrange("(p c) j -> p c j", c=out_blocks)
     with (
         tc.tile_pool(name="held", bufs=1) as held,
         tc.psum_pool(name="psum", bufs=1) as psum,
@@ -38,25 +40,32 @@ def tile_lookup_steptanh_relu_kernel(tc, tab, w, b, offs, out):
             keys.append(key)
             values.append(value)
 
-        sums = [psum.tile([P, PICKS], F32, name=f"sums{c}") for c in range(out_blocks)]
+        sums = [
+            [psum.tile([P, PART], F32, name=f"sums{h}_{c}") for c in range(out_blocks)]
+            for h in range(PARTS)
+        ]
         for r in range(row_blocks):
-            gate = held.tile([P, PICKS], F32, name=f"gate{r}")
-            squashed = held.tile([P, PICKS], F32, name=f"squashed{r}")
-            x = held.tile([P, PICKS], BF16, name=f"x{r}")
-            nc.vector.tensor_scalar(gate[:], keys[r][:].indirect(offsets[:]), THRESHOLD, GAIN, ALU.is_ge, ALU.mult)
-            nc.scalar.activation(squashed[:], values[r][:].indirect(offsets[:]), ACT.Tanh)
-            nc.vector.tensor_tensor(x[:], gate[:], squashed[:], ALU.mult)
-            for c in range(out_blocks):
-                nc.tensor.matmul(
-                    sums[c][:], weights[:, r, c::out_blocks], x[:],
-                    start=(r == 0), stop=(r == row_blocks - 1),
+            for h in range(PARTS):
+                part_offsets = offsets[:, h * PART // 16 : (h + 1) * PART // 16]
+                gate = held.tile([P, PART], F32, name=f"gate{r}_{h}")
+                squashed = held.tile([P, PART], F32, name=f"squashed{r}_{h}")
+                x = held.tile([P, PART], BF16, name=f"x{r}_{h}")
+                nc.vector.tensor_scalar(
+                    gate[:], keys[r][:].indirect(part_offsets), THRESHOLD, GAIN, ALU.is_ge, ALU.mult
                 )
+                nc.scalar.activation(squashed[:], values[r][:].indirect(part_offsets), ACT.Tanh)
+                nc.vector.tensor_tensor(x[:], gate[:], squashed[:], ALU.mult)
+                for c in range(out_blocks):
+                    nc.tensor.matmul(
+                        sums[h][c][:], weights[:, r, c::out_blocks], x[:],
+                        start=(r == 0), stop=(r == row_blocks - 1),
+                    )
 
-        for c in range(out_blocks):
-            result = held.tile([P, PICKS], F32, name=f"result{c}")
-            bias_c = bias[:, c : c + 1]
-            if c % 2 == 0:
-                nc.scalar.activation(result[:], sums[c][:], ACT.Relu, bias=bias_c)
-            else:
-                nc.vector.tensor_scalar(result[:], sums[c][:], bias_c, 0.0, ALU.add, ALU.max)
-            nc.sync.dma_start(out_by_block[c], result[:])
+        for h in range(PARTS):
+            for c in range(0, out_blocks, 2):
+                result = held.tile([P, 2, PART], F32, name=f"result{h}_{c}")
+                nc.scalar.activation(result[:, 0, :], sums[h][c][:], ACT.Relu, bias=bias[:, c : c + 1])
+                nc.vector.tensor_scalar(
+                    result[:, 1, :], sums[h][c + 1][:], bias[:, c + 1 : c + 2], 0.0, ALU.add, ALU.max
+                )
+                nc.sync.dma_start(out_by_part[:, c : c + 2, h * PART : (h + 1) * PART], result[:])

@@ -22,23 +22,18 @@ def tile_lookup_steptanh_relu_kernel(tc, tab, w, b, offs, out):
         tc.tile_pool(name="held", bufs=1) as held,
         tc.psum_pool(name="psum", bufs=1) as psum,
     ):
+        keys = [held.tile([P, PLACES], F32, name=f"key{r}") for r in range(row_blocks)]
+        values = [held.tile([P, PLACES], F32, name=f"value{r}") for r in range(row_blocks)]
         offsets = held.tile([P, PICKS // 16], U16, name="offsets")
-        nc.sync.dma_start(offsets[:], offs)
-
         weights = held.tile([P, row_blocks, OUTS], BF16, name="weights")
         bias = held.tile([P, out_blocks], F32, name="bias")
-        keys, values = [], []
+        nc.sync.dma_start(offsets[:], offs)
         for r in range(row_blocks):
-            rows = slice(r * P, (r + 1) * P)
-            key = held.tile([P, PLACES], F32, name=f"key{r}")
-            value = held.tile([P, PLACES], F32, name=f"value{r}")
-            nc.sync.dma_start(key[:], tab[0, rows, :])
-            nc.sync.dma_start(value[:], tab[1, rows, :])
-            if r == 0:
-                nc.sync.dma_start(weights[:], w.rearrange("(r p) m -> p r m", p=P))
-                nc.sync.dma_start(bias[:], b.rearrange("(p c) one -> p (c one)", c=out_blocks))
-            keys.append(key)
-            values.append(value)
+            nc.sync.dma_start(keys[r][:], tab[0, r * P : (r + 1) * P, :])
+        nc.sync.dma_start(weights[:], w.rearrange("(r p) m -> p r m", p=P))
+        nc.sync.dma_start(bias[:], b.rearrange("(p c) one -> p (c one)", c=out_blocks))
+        for r in range(row_blocks):
+            nc.sync.dma_start(values[r][:], tab[1, r * P : (r + 1) * P, :])
 
         sums = [
             [psum.tile([P, PART], F32, name=f"sums{h}_{c}") for c in range(out_blocks)]

@@ -22,6 +22,11 @@ def tile_lookup_steptanh_relu_kernel(tc, tab, w, b, offs, out):
         tc.tile_pool(name="held", bufs=1) as held,
         tc.psum_pool(name="psum", bufs=1) as psum,
     ):
+        zeros = held.tile([P, 1], F32, name="zeros")
+        tables_loaded = held.tile([P, 1], F32, name="tables_loaded")
+        nc.vector.memset(zeros[:], 0.0)
+        nc.scalar.activation(tables_loaded[:], zeros[:], ACT.Tanh)
+
         keys = [held.tile([P, PLACES], F32, name=f"key{r}") for r in range(row_blocks)]
         values = [held.tile([P, PLACES], F32, name=f"value{r}") for r in range(row_blocks)]
         offsets = held.tile([P, PICKS // 16], U16, name="offsets")
@@ -57,10 +62,11 @@ def tile_lookup_steptanh_relu_kernel(tc, tab, w, b, offs, out):
                     )
 
         for h in range(PARTS):
-            for c in range(0, out_blocks, 2):
-                result = held.tile([P, 2, PART], F32, name=f"result{h}_{c}")
-                nc.scalar.activation(result[:, 0, :], sums[h][c][:], ACT.Relu, bias=bias[:, c : c + 1])
-                nc.vector.tensor_scalar(
-                    result[:, 1, :], sums[h][c + 1][:], bias[:, c + 1 : c + 2], 0.0, ALU.add, ALU.max
-                )
-                nc.sync.dma_start(out_by_part[:, c : c + 2, h * PART : (h + 1) * PART], result[:])
+            for c in range(out_blocks):
+                result = held.tile([P, PART], F32, name=f"result{h}_{c}")
+                bias_c = bias[:, c : c + 1]
+                if c % 2 == 0:
+                    nc.scalar.activation(result[:], sums[h][c][:], ACT.Relu, bias=bias_c)
+                else:
+                    nc.vector.tensor_scalar(result[:], sums[h][c][:], bias_c, 0.0, ALU.add, ALU.max)
+                nc.sync.dma_start(out_by_part[:, c, h * PART : (h + 1) * PART], result[:])

import concourse.mybir as mybir

BF16, F32, U16 = mybir.dt.bfloat16, mybir.dt.float32, mybir.dt.uint16
ALU = mybir.AluOpType
ACT = mybir.ActivationFunctionType

P = 128
ROWS, PLACES = 256, 2048
PICKS, OUTS = 512, 512
PARTS = 2
PART = PICKS // PARTS
THRESHOLD, GAIN = 0.25, 0.5
FLOPS = 2 * ROWS * OUTS * PICKS


def tile_lookup_steptanh_relu_kernel(tc, tab, w, b, offs, out):
    nc = tc.nc
    row_blocks = ROWS // P
    out_blocks = OUTS // P
    out_by_part = out.rearrange("(p c) j -> p c j", c=out_blocks)
    with (
        tc.tile_pool(name="held", bufs=1) as held,
        tc.psum_pool(name="psum", bufs=1) as psum,
    ):
        zeros = held.tile([P, 1], F32, name="zeros")
        tables_loaded = held.tile([P, 1], F32, name="tables_loaded")
        nc.vector.memset(zeros[:], 0.0)
        nc.scalar.activation(tables_loaded[:], zeros[:], ACT.Tanh)

        keys = [held.tile([P, PLACES], F32, name=f"key{r}") for r in range(row_blocks)]
        values = [held.tile([P, PLACES], F32, name=f"value{r}") for r in range(row_blocks)]
        offsets = held.tile([P, PICKS // 16], U16, name="offsets")
        weights = held.tile([P, row_blocks, OUTS], BF16, name="weights")
        bias = held.tile([P, out_blocks], F32, name="bias")
        nc.sync.dma_start(offsets[:], offs)
        for r in range(row_blocks):
            nc.sync.dma_start(keys[r][:], tab[0, r * P : (r + 1) * P, :])
        nc.sync.dma_start(weights[:], w.rearrange("(r p) m -> p r m", p=P))
        nc.sync.dma_start(bias[:], b.rearrange("(p c) one -> p (c one)", c=out_blocks))
        for r in range(row_blocks):
            nc.sync.dma_start(values[r][:], tab[1, r * P : (r + 1) * P, :])

        sums = [
            [psum.tile([P, PART], F32, name=f"sums{h}_{c}") for c in range(out_blocks)]
            for h in range(PARTS)
        ]
        for r in range(row_blocks):
            for h in range(PARTS):
                part_offsets = offsets[:, h * PART // 16 : (h + 1) * PART // 16]
                gate = held.tile([P, PART], F32, name=f"gate{r}_{h}")
                squashed = held.tile([P, PART], F32, name=f"squashed{r}_{h}")
                x = held.tile([P, PART], BF16, name=f"x{r}_{h}")
                nc.vector.tensor_scalar(
                    gate[:], keys[r][:].indirect(part_offsets), THRESHOLD, GAIN, ALU.is_ge, ALU.mult
                )
                nc.scalar.activation(squashed[:], values[r][:].indirect(part_offsets), ACT.Tanh)
                nc.vector.tensor_tensor(x[:], gate[:], squashed[:], ALU.mult)
                for c in range(out_blocks):
                    nc.tensor.matmul(
                        sums[h][c][:], weights[:, r, c::out_blocks], x[:],
                        start=(r == 0), stop=(r == row_blocks - 1),
                    )

        for h in range(PARTS):
            for c in range(out_blocks):
                result = held.tile([P, PART], F32, name=f"result{h}_{c}")
                bias_c = bias[:, c : c + 1]
                if c % 2 == 0:
                    nc.scalar.activation(result[:], sums[h][c][:], ACT.Relu, bias=bias_c)
                else:
                    nc.vector.tensor_scalar(result[:], sums[h][c][:], bias_c, 0.0, ALU.add, ALU.max)
                nc.sync.dma_start(out_by_part[:, c, h * PART : (h + 1) * PART], result[:])
